import numpy as np
import ml_dtypes


def mxq(x, axis, fmt="e4m3"):
    dtype, down = {"e4m3": (ml_dtypes.float8_e4m3fn, 7), "e5m2": (ml_dtypes.float8_e5m2, 14)}[fmt]
    v = np.moveaxis(np.asarray(x, np.float32).astype(ml_dtypes.bfloat16).astype(np.float64), axis, -1)
    blocks = v.reshape(v.shape[:-1] + (-1, 32))
    amax = np.abs(blocks).max(-1, keepdims=True)
    byte = np.maximum(np.where(amax > 0, np.frexp(amax)[1] - 1 + 127, 0) - down, 1)
    scale = np.exp2(byte - 127.0)
    codes = (blocks / scale).astype(np.float32).astype(dtype).astype(np.float64)
    return np.moveaxis((codes * scale).reshape(v.shape), -1, axis)


WIDE = False


def mx_kscale(k):
    if not WIDE:
        return np.ones(k)
    levels = np.array([10, -10, 5, -5, 0])
    if k % 512:
        return np.exp2(np.random.permutation(np.resize(levels, k // 32))).repeat(32)
    a = np.empty((k // 512, 16))
    for p in range(k // 512):
        a[p, :8] = np.random.permutation(np.resize(levels, 8))
        for g in range(8):
            far = levels[np.abs(levels - a[p, g]) >= 10]
            a[p, g + 8] = far[np.random.randint(len(far))]
    return np.exp2(a.ravel()).repeat(32)


def f64(x):
    return np.asarray(x).astype(np.float64)


def striped8(idx):
    return np.asarray(idx).reshape(8, -1, 16).transpose(0, 2, 1).reshape(128, -1).astype(np.uint16)


def unstriped8(offs):
    return offs.reshape(8, 16, -1).transpose(0, 2, 1).reshape(8, -1).astype(np.int64)


def pick8(x, idx, run):
    r = np.arange(len(x))
    return x[r[:, None], idx[r % (8 * run) // run]]


E2M1 = np.array([0.0, 0.5, 1.0, 1.5, 2.0, 3.0, 4.0, 6.0, -0.0, -0.5, -1.0, -1.5, -2.0, -3.0, -4.0, -6.0])


def pack_weight(w, fmt):
    k, n = w.shape
    w = f64(np.asarray(w, np.float32).astype(ml_dtypes.bfloat16)).reshape(k // 32, 32, n)
    amax = np.abs(w).max(1)
    if fmt == "e4m3":
        byte = np.frexp(amax)[1] - 1 + 127 - 7
    else:
        mant, ex = np.frexp(amax / 6.0)
        byte = np.where(mant > 0.5, ex, ex - 1) + 127
    byte = np.clip(np.where(amax > 0, byte, 1), 1, 254)
    scaled = (w * np.exp2(127.0 - byte)[:, None, :]).reshape(k, n).astype(np.float32)
    by_word = np.ascontiguousarray(scaled.reshape(k // 512, 128, 4, n).transpose(0, 1, 3, 2))
    if fmt == "e4m3":
        words = by_word.astype(ml_dtypes.float8_e4m3fn).view(np.uint8)
    else:
        c = by_word.astype(ml_dtypes.float4_e2m1fn).view(np.uint8) & 0xF
        words = (c[..., 0::2] | (c[..., 1::2] << 4)).reshape(k // 512, 128, 2 * n)
    return np.ascontiguousarray(words), np.ascontiguousarray(byte.astype(np.uint8).reshape(k // 512, 16, n))


def unpack_weight(words, scales, fmt):
    g, _, n = scales.shape
    words = np.ascontiguousarray(words).reshape(g, 128, n, -1)
    if fmt == "e4m3":
        vals = words.view(ml_dtypes.float8_e4m3fn).astype(np.float64)
    else:
        nib = np.empty((g, 128, n, 4), np.uint8)
        nib[..., 0::2] = words & 0xF
        nib[..., 1::2] = words >> 4
        vals = E2M1[nib]
    vals = vals * np.repeat(np.exp2(scales.astype(np.float64) - 127.0), 8, axis=1)[..., None]
    return vals.transpose(0, 1, 3, 2).reshape(g * 512, n)


K, T, J, L, N = 512, 1024, 512, 512, 512


def setup_inputs():
    n = np.random.standard_normal
    idx = np.stack([np.random.permutation(T)[:J] for _ in range(8)])
    idx2 = np.stack([np.random.permutation(T)[:J] for _ in range(8)])
    fk = mx_kscale(K)
    fl = mx_kscale(L)
    wp = pack_weight(n((K, N)) * 1 / np.sqrt(K) * fk[:, None], "e2m1")
    bxp = pack_weight(n((L, J)) / fl[:, None], "e4m3")
    wbp = pack_weight(n((L, N)) * 1 / np.sqrt(L) * fl[:, None], "e2m1")
    return {
        "xf": (n((K, T)) / fk[:, None]).astype(np.float32),
        "w_words": wp[0],
        "w_scales": wp[1],
        "bx_words": bxp[0],
        "bx_scales": bxp[1],
        "wb_words": wbp[0],
        "wb_scales": wbp[1],
        "offs": striped8(idx),
        "offs2": striped8(idx2),
    }


def reference(xf, w_words, w_scales, bx_words, bx_scales, wb_words, wb_scales, offs, offs2):
    idx = unstriped8(offs)
    idx2 = unstriped8(offs2)
    wu = unpack_weight(w_words, w_scales, "e2m1")
    bxu = unpack_weight(bx_words, bx_scales, "e4m3")
    wbu = unpack_weight(wb_words, wb_scales, "e2m1")
    d = pick8(f64(xf), idx, 64) - pick8(f64(xf), idx2, 64)
    dq = mxq(d, 0, "e4m3")
    y = wu.T @ dq + wbu.T @ bxu
    return y

@@ -1,0 +1,147 @@
+from contextlib import ExitStack
+
+import concourse.mybir as mybir
+
+K, T, J, L, N = 512, 1024, 512, 512, 512
+FLOPS = 2 * K * N * J + 2 * L * N * J
+
+F32 = mybir.dt.float32
+BF16 = mybir.dt.bfloat16
+I32 = mybir.dt.int32
+U32 = mybir.dt.uint32
+U16 = mybir.dt.uint16
+U8 = mybir.dt.uint8
+FP8X4 = mybir.dt.float8_e4m3fn_x4
+FP4X4 = mybir.dt.float4_e2m1fn_x4
+SUBTRACT = mybir.AluOpType.subtract
+
+P = 128
+PACK = 4
+HALF = J // 2
+CHUNK = 128
+LIST_COLS = HALF // 16
+
+
+def tile_list_head_changes_in_kernel(
+    tc, xf, w_words, w_scales, bx_words, bx_scales, wb_words, wb_scales, offs, offs2, out
+):
+    nc = tc.nc
+    with ExitStack() as ctx:
+        sb = ctx.enter_context(tc.tile_pool(name="sb", bufs=1))
+        ps = ctx.enter_context(tc.psum_pool(name="ps", bufs=1))
+
+        lists = sb.tile([P, J // 16], U16, name="lists")
+        lists2 = sb.tile([P, J // 16], U16, name="lists2")
+        x = [sb.tile([P, T], F32, name=f"x{t}") for t in range(PACK)]
+        w_codes = sb.tile([P, 2 * N], U8, name="w_codes", align_bytes=64)
+        wb_codes = sb.tile([P, 2 * N], U8, name="wb_codes", align_bytes=64)
+        bx_codes = sb.tile([P, J], U32, name="bx_codes", align_bytes=64)
+        w_plane = sb.tile([P, N], U8, name="w_plane", align_bytes=64)
+        wb_plane = sb.tile([P, N], U8, name="wb_plane", align_bytes=64)
+        bx_plane = sb.tile([P, J], U8, name="bx_plane", align_bytes=64)
+
+        for plane in (wb_plane, bx_plane, w_plane):
+            nc.vector.memset(plane[:].bitcast(I32), 0)
+
+        x_rows = xf.rearrange("(p t) c -> p t c", t=PACK)
+        nc.sync.dma_start(lists2[:], offs2)
+        nc.sync.dma_start(x[0][:], x_rows[:, 0, :])
+        nc.sync.dma_start(lists[:], offs)
+        for t in range(1, PACK):
+            nc.sync.dma_start(x[t][:], x_rows[:, t, :])
+        nc.sync.dma_start(wb_codes[:].bitcast(I32), wb_words[0].bitcast(I32))
+        nc.sync.dma_start(bx_codes[:].bitcast(I32), bx_words[0].rearrange("p c r -> p (c r)").bitcast(I32))
+        nc.sync.dma_start(w_codes[:].bitcast(I32), w_words[0].bitcast(I32))
+        for plane, scales in ((wb_plane, wb_scales), (bx_plane, bx_scales), (w_plane, w_scales)):
+            for q in range(4):
+                nc.sync.dma_start(
+                    plane[32 * q : 32 * q + 4, :].bitcast(I32), scales[0, 4 * q : 4 * q + 4, :].bitcast(I32)
+                )
+
+        slots = sb.tile([P, 6 * HALF], F32, name="slots")
+
+        def slot(s, count=1):
+            return slots[:, s * HALF : (s + count) * HALF]
+
+        def cut(tile, half):
+            return tile[:, half * LIST_COLS : (half + 1) * LIST_COLS]
+
+        second = [
+            [sb.tile([P, HALF], F32, name=f"second0_{t}")[:] for t in range(PACK - 1)] + [slot(4)],
+            [sb.tile([P, HALF], F32, name=f"second1_{t}")[:] for t in range(PACK)],
+        ]
+
+        def pick_second(half, t):
+            nc.vector.tensor_copy(second[half][t], x[t][:].indirect(cut(lists2, half)))
+
+        def change(half, t):
+            nc.vector.tensor_tensor(slot(2 * half + t), x[t][:].indirect(cut(lists, half)), second[half][t], SUBTRACT)
+
+        woven = [sb.tile([P, HALF, PACK], BF16, name=f"woven{h}", align_bytes=64) for h in range(2)]
+
+        def weave(copy, half, pair, j0, j1):
+            src = slot(2 * half + 2 * pair, 2).rearrange("p (t j) -> p j t", t=2)
+            copy(woven[half][:, j0:j1, 2 * pair : 2 * pair + 2], src[:, j0:j1, :])
+
+        def quantise(half, j0, j1):
+            codes = sb.tile([P, j1 - j0], U32, name=f"d_codes{half}_{j0}", align_bytes=64)
+            plane = sb.tile([P, j1 - j0], U8, name=f"d_plane{half}_{j0}", align_bytes=64)
+            nc.vector.quantize_mx(
+                out=codes[:].bitcast(FP8X4),
+                scales=plane[:],
+                in_=woven[half][:, j0:j1, :].rearrange("p j t -> p (j t)"),
+            )
+            return codes, plane
+
+        banks = {}
+        for c in range(J // CHUNK):
+            for g in range(2):
+                banks[c, g] = ps.tile([P, 2, CHUNK], F32, name=f"bank{c}_{g}")
+
+        def product(c, codes, plane, rhs, rhs_plane, first):
+            for m in range(N // P):
+                nc.tensor.matmul_mx(
+                    out=banks[c, m // 2][:, m % 2, :],
+                    lhsT=codes[:, 2 * P * m : 2 * P * (m + 1)].bitcast(FP4X4),
+                    lhsT_scale=plane[:, P * m : P * (m + 1)],
+                    rhs=rhs.bitcast(FP8X4),
+                    rhs_scale=rhs_plane,
+                    start=first and m % 2 == 0,
+                    stop=(not first) and m % 2 == 1,
+                )
+
+        for c in range(J // CHUNK):
+            cols = slice(c * CHUNK, (c + 1) * CHUNK)
+            product(c, wb_codes, wb_plane, bx_codes[:, cols], bx_plane[:, cols], True)
+
+        out_rows = out.rearrange("(m p) j -> p m j", p=P)
+
+        def finish(half, copies, queues):
+            for g in range(2):
+                result = sb.tile([P, 2, HALF], F32, name=f"result{half}_{g}")
+                for c in range(2):
+                    copies[g](result[:, :, c * CHUNK : (c + 1) * CHUNK], banks[2 * half + c, g][:])
+                queues[g].dma_start(out_rows[:, 2 * g : 2 * g + 2, half * HALF : (half + 1) * HALF], result[:])
+
+        for t in range(PACK):
+            pick_second(0, t)
+            pick_second(1, t)
+            change(0, t)
+            if t % 2 == 1:
+                weave(nc.scalar.copy, 0, t // 2, 0, HALF)
+        change(1, 3)
+        change(1, 2)
+        weave(nc.scalar.copy, 1, 1, 0, HALF)
+        codes, plane = quantise(0, 0, HALF)
+        for c in range(2):
+            cols = slice(c * CHUNK, (c + 1) * CHUNK)
+            product(c, w_codes, w_plane, codes[:, cols], plane[:, cols], False)
+        change(1, 0)
+        change(1, 1)
+        finish(0, (nc.scalar.copy, nc.scalar.copy), (nc.sync, nc.sync))
+        for c in range(2):
+            weave(nc.vector.tensor_copy, 1, 0, c * CHUNK, (c + 1) * CHUNK)
+        for c in range(2):
+            codes, plane = quantise(1, c * CHUNK, (c + 1) * CHUNK)
+            product(2 + c, w_codes, w_plane, codes[:], plane[:], False)
+        finish(1, (nc.vector.tensor_copy, nc.scalar.copy), (nc.sync, nc.scalar))

@@ -35,7 +35,6 @@ def tile_list_head_changes_in_kernel(
         x = [sb.tile([P, T], F32, name=f"x{t}") for t in range(PACK)]
         w_codes = sb.tile([P, 2 * N], U8, name="w_codes", align_bytes=64)
         wb_codes = sb.tile([P, 2 * N], U8, name="wb_codes", align_bytes=64)
-        bx_codes = sb.tile([P, J], U32, name="bx_codes", align_bytes=64)
         w_plane = sb.tile([P, N], U8, name="w_plane", align_bytes=64)
         wb_plane = sb.tile([P, N], U8, name="wb_plane", align_bytes=64)
         bx_plane = sb.tile([P, J], U8, name="bx_plane", align_bytes=64)
@@ -43,31 +42,34 @@ def tile_list_head_changes_in_kernel(
         for plane in (wb_plane, bx_plane, w_plane):
             nc.vector.memset(plane[:].bitcast(I32), 0)
 
-        x_rows = xf.rearrange("(p t) c -> p t c", t=PACK)
-        nc.sync.dma_start(lists2[:], offs2)
-        nc.sync.dma_start(x[0][:], x_rows[:, 0, :])
-        nc.sync.dma_start(lists[:], offs)
-        for t in range(1, PACK):
-            nc.sync.dma_start(x[t][:], x_rows[:, t, :])
-        nc.sync.dma_start(wb_codes[:].bitcast(I32), wb_words[0].bitcast(I32))
-        nc.sync.dma_start(bx_codes[:].bitcast(I32), bx_words[0].rearrange("p c r -> p (c r)").bitcast(I32))
-        nc.sync.dma_start(w_codes[:].bitcast(I32), w_words[0].bitcast(I32))
-        for plane, scales in ((wb_plane, wb_scales), (bx_plane, bx_scales), (w_plane, w_scales)):
+        def load_plane(plane, scales):
             for q in range(4):
                 nc.sync.dma_start(
                     plane[32 * q : 32 * q + 4, :].bitcast(I32), scales[0, 4 * q : 4 * q + 4, :].bitcast(I32)
                 )
 
-        slots = sb.tile([P, 6 * HALF], F32, name="slots")
-
-        def slot(s, count=1):
-            return slots[:, s * HALF : (s + count) * HALF]
+        x_rows = xf.rearrange("(p t) c -> p t c", t=PACK)
+        nc.sync.dma_start(x[0][:], x_rows[:, 0, :])
+        nc.sync.dma_start(lists2[:], offs2)
+        nc.sync.dma_start(lists[:], offs)
+        nc.sync.dma_start(x[1][:], x_rows[:, 1, :])
+        load_plane(wb_plane, wb_scales)
+        nc.sync.dma_start(x[2][:], x_rows[:, 2, :])
+        load_plane(bx_plane, bx_scales)
+        nc.sync.dma_start(x[3][:], x_rows[:, 3, :])
+        nc.sync.dma_start(wb_codes[:].bitcast(I32), wb_words[0].bitcast(I32))
+        load_plane(w_plane, w_scales)
+        nc.sync.dma_start(w_codes[:].bitcast(I32), w_words[0].bitcast(I32))
 
         def cut(tile, half):
             return tile[:, half * LIST_COLS : (half + 1) * LIST_COLS]
 
+        low0 = sb.tile([P, 2, HALF], F32, name="low0", align_bytes=64)
+        shared = sb.tile([P, 2, HALF], F32, name="shared")
+        high1 = sb.tile([P, 2, HALF], F32, name="high1")
+        pairs = [[low0, shared], [shared, high1]]
         second = [
-            [sb.tile([P, HALF], F32, name=f"second0_{t}")[:] for t in range(PACK - 1)] + [slot(4)],
+            [sb.tile([P, HALF], F32, name=f"second0_{t}")[:] for t in range(PACK - 1)] + [high1[:, 0, :]],
             [sb.tile([P, HALF], F32, name=f"second1_{t}")[:] for t in range(PACK)],
         ]
 
@@ -75,12 +77,14 @@ def tile_list_head_changes_in_kernel(
             nc.vector.tensor_copy(second[half][t], x[t][:].indirect(cut(lists2, half)))
 
         def change(half, t):
-            nc.vector.tensor_tensor(slot(2 * half + t), x[t][:].indirect(cut(lists, half)), second[half][t], SUBTRACT)
+            nc.vector.tensor_tensor(
+                pairs[half][t // 2][:, t % 2, :], x[t][:].indirect(cut(lists, half)), second[half][t], SUBTRACT
+            )
 
         woven = [sb.tile([P, HALF, PACK], BF16, name=f"woven{h}", align_bytes=64) for h in range(2)]
 
         def weave(copy, half, pair, j0, j1):
-            src = slot(2 * half + 2 * pair, 2).rearrange("p (t j) -> p j t", t=2)
+            src = pairs[half][pair][:].rearrange("p t j -> p j t")
             copy(woven[half][:, j0:j1, 2 * pair : 2 * pair + 2], src[:, j0:j1, :])
 
         def quantise(half, j0, j1):
@@ -93,15 +97,12 @@ def tile_list_head_changes_in_kernel(
             )
             return codes, plane
 
-        banks = {}
-        for c in range(J // CHUNK):
-            for g in range(2):
-                banks[c, g] = ps.tile([P, 2, CHUNK], F32, name=f"bank{c}_{g}")
+        banks = {(c, g): ps.tile([P, 2, CHUNK], F32, name=f"bank{c}_{g}") for c in range(4) for g in range(2)}
 
-        def product(c, codes, plane, rhs, rhs_plane, first):
-            for m in range(N // P):
+        def product(c, g, codes, plane, rhs, rhs_plane, first):
+            for m in (2 * g, 2 * g + 1):
                 nc.tensor.matmul_mx(
-                    out=banks[c, m // 2][:, m % 2, :],
+                    out=banks[c, g][:, m % 2, :],
                     lhsT=codes[:, 2 * P * m : 2 * P * (m + 1)].bitcast(FP4X4),
                     lhsT_scale=plane[:, P * m : P * (m + 1)],
                     rhs=rhs.bitcast(FP8X4),
@@ -109,10 +110,6 @@ def tile_list_head_changes_in_kernel(
                     start=first and m % 2 == 0,
                     stop=(not first) and m % 2 == 1,
                 )
-
-        for c in range(J // CHUNK):
-            cols = slice(c * CHUNK, (c + 1) * CHUNK)
-            product(c, wb_codes, wb_plane, bx_codes[:, cols], bx_plane[:, cols], True)
 
         out_rows = out.rearrange("(m p) j -> p m j", p=P)
 
@@ -129,13 +126,20 @@ def tile_list_head_changes_in_kernel(
             change(0, t)
             if t % 2 == 1:
                 weave(nc.scalar.copy, 0, t // 2, 0, HALF)
+        bx_codes = sb.tile([P, J], U32, name="bx_codes", tag="low0", align_bytes=64)
+        nc.scalar.dma_start(bx_codes[:].bitcast(I32), bx_words[0].rearrange("p c r -> p (c r)").bitcast(I32))
+        for c in range(4):
+            for g in range(2):
+                cols = slice(c * CHUNK, (c + 1) * CHUNK)
+                product(c, g, wb_codes, wb_plane, bx_codes[:, cols], bx_plane[:, cols], True)
         change(1, 3)
         change(1, 2)
         weave(nc.scalar.copy, 1, 1, 0, HALF)
         codes, plane = quantise(0, 0, HALF)
-        for c in range(2):
-            cols = slice(c * CHUNK, (c + 1) * CHUNK)
-            product(c, w_codes, w_plane, codes[:, cols], plane[:, cols], False)
+        for g in range(2):
+            for c in range(2):
+                cols = slice(c * CHUNK, (c + 1) * CHUNK)
+                product(c, g, w_codes, w_plane, codes[:, cols], plane[:, cols], False)
         change(1, 0)
         change(1, 1)
         finish(0, (nc.scalar.copy, nc.scalar.copy), (nc.sync, nc.sync))
@@ -143,5 +147,6 @@ def tile_list_head_changes_in_kernel(
             weave(nc.vector.tensor_copy, 1, 0, c * CHUNK, (c + 1) * CHUNK)
         for c in range(2):
             codes, plane = quantise(1, c * CHUNK, (c + 1) * CHUNK)
-            product(2 + c, w_codes, w_plane, codes[:], plane[:], False)
+            for g in range(2):
+                product(2 + c, g, w_codes, w_plane, codes[:], plane[:], False)
         finish(1, (nc.vector.tensor_copy, nc.scalar.copy), (nc.sync, nc.scalar))

@@ -65,12 +65,12 @@ def tile_list_head_changes_in_kernel(
             return tile[:, half * LIST_COLS : (half + 1) * LIST_COLS]
 
         low0 = sb.tile([P, 2, HALF], F32, name="low0", align_bytes=64)
-        shared = sb.tile([P, 2, HALF], F32, name="shared")
+        shared = sb.tile([P, 3, HALF], F32, name="shared")
         high1 = sb.tile([P, 2, HALF], F32, name="high1")
-        pairs = [[low0, shared], [shared, high1]]
+        pairs = [[low0[:], shared[:, 1:3, :]], [shared[:, 0:2, :], high1[:]]]
         second = [
             [sb.tile([P, HALF], F32, name=f"second0_{t}")[:] for t in range(PACK - 1)] + [high1[:, 0, :]],
-            [sb.tile([P, HALF], F32, name=f"second1_{t}")[:] for t in range(PACK)],
+            [sb.tile([P, HALF], F32, name=f"second1_{t}")[:] for t in range(PACK - 1)] + [shared[:, 0, :]],
         ]
 
         def pick_second(half, t):
@@ -84,7 +84,7 @@ def tile_list_head_changes_in_kernel(
         woven = [sb.tile([P, HALF, PACK], BF16, name=f"woven{h}", align_bytes=64) for h in range(2)]
 
         def weave(copy, half, pair, j0, j1):
-            src = pairs[half][pair][:].rearrange("p t j -> p j t")
+            src = pairs[half][pair].rearrange("p t j -> p j t")
             copy(woven[half][:, j0:j1, 2 * pair : 2 * pair + 2], src[:, j0:j1, :])
 
         def quantise(half, j0, j1):
@@ -97,28 +97,23 @@ def tile_list_head_changes_in_kernel(
             )
             return codes, plane
 
-        banks = {(c, g): ps.tile([P, 2, CHUNK], F32, name=f"bank{c}_{g}") for c in range(4) for g in range(2)}
+        banks = {(h, m): ps.tile([P, HALF], F32, name=f"bank{h}_{m}") for h in range(2) for m in range(N // P)}
 
-        def product(c, g, codes, plane, rhs, rhs_plane, first):
-            for m in (2 * g, 2 * g + 1):
-                nc.tensor.matmul_mx(
-                    out=banks[c, g][:, m % 2, :],
-                    lhsT=codes[:, 2 * P * m : 2 * P * (m + 1)].bitcast(FP4X4),
-                    lhsT_scale=plane[:, P * m : P * (m + 1)],
-                    rhs=rhs.bitcast(FP8X4),
-                    rhs_scale=rhs_plane,
-                    start=first and m % 2 == 0,
-                    stop=(not first) and m % 2 == 1,
-                )
+        def product(half, m, c, codes, plane, rhs, rhs_plane, first):
+            nc.tensor.matmul_mx(
+                out=banks[half, m][:, c * CHUNK : (c + 1) * CHUNK],
+                lhsT=codes[:, 2 * P * m : 2 * P * (m + 1)].bitcast(FP4X4),
+                lhsT_scale=plane[:, P * m : P * (m + 1)],
+                rhs=rhs.bitcast(FP8X4),
+                rhs_scale=rhs_plane,
+                start=first and c == 0,
+                stop=(not first) and c == 1,
+            )
 
-        out_rows = out.rearrange("(m p) j -> p m j", p=P)
-
-        def finish(half, copies, queues):
-            for g in range(2):
-                result = sb.tile([P, 2, HALF], F32, name=f"result{half}_{g}")
-                for c in range(2):
-                    copies[g](result[:, :, c * CHUNK : (c + 1) * CHUNK], banks[2 * half + c, g][:])
-                queues[g].dma_start(out_rows[:, 2 * g : 2 * g + 2, half * HALF : (half + 1) * HALF], result[:])
+        def finish(half, m, copy, queue):
+            result = sb.tile([P, HALF], F32, name=f"result{half}_{m}")
+            copy(result[:], banks[half, m][:])
+            queue.dma_start(out[m * P : (m + 1) * P, half * HALF : (half + 1) * HALF], result[:])
 
         for t in range(PACK):
             pick_second(0, t)
@@ -128,25 +123,29 @@ def tile_list_head_changes_in_kernel(
                 weave(nc.scalar.copy, 0, t // 2, 0, HALF)
         bx_codes = sb.tile([P, J], U32, name="bx_codes", tag="low0", align_bytes=64)
         nc.scalar.dma_start(bx_codes[:].bitcast(I32), bx_words[0].rearrange("p c r -> p (c r)").bitcast(I32))
-        for c in range(4):
-            for g in range(2):
-                cols = slice(c * CHUNK, (c + 1) * CHUNK)
-                product(c, g, wb_codes, wb_plane, bx_codes[:, cols], bx_plane[:, cols], True)
+        for half in range(2):
+            for m in range(N // P):
+                for c in range(2):
+                    cols = slice(half * HALF + c * CHUNK, half * HALF + (c + 1) * CHUNK)
+                    product(half, m, c, wb_codes, wb_plane, bx_codes[:, cols], bx_plane[:, cols], True)
         change(1, 3)
         change(1, 2)
         weave(nc.scalar.copy, 1, 1, 0, HALF)
+        change(1, 0)
         codes, plane = quantise(0, 0, HALF)
-        for g in range(2):
+        for m in range(N // P):
             for c in range(2):
                 cols = slice(c * CHUNK, (c + 1) * CHUNK)
-                product(c, g, w_codes, w_plane, codes[:, cols], plane[:, cols], False)
-        change(1, 0)
+                product(0, m, c, w_codes, w_plane, codes[:, cols], plane[:, cols], False)
+            finish(0, m, nc.scalar.copy, nc.sync)
         change(1, 1)
-        finish(0, (nc.scalar.copy, nc.scalar.copy), (nc.sync, nc.sync))
         for c in range(2):
             weave(nc.vector.tensor_copy, 1, 0, c * CHUNK, (c + 1) * CHUNK)
-        for c in range(2):
-            codes, plane = quantise(1, c * CHUNK, (c + 1) * CHUNK)
-            for g in range(2):
-                product(2 + c, g, w_codes, w_plane, codes[:], plane[:], False)
-        finish(1, (nc.vector.tensor_copy, nc.scalar.copy), (nc.sync, nc.scalar))
+        last = [quantise(1, c * CHUNK, (c + 1) * CHUNK) for c in range(2)]
+        for m in range(N // P):
+            for c in range(2):
+                product(1, m, c, w_codes, w_plane, last[c][0][:], last[c][1][:], False)
+            if m % 2 == 0:
+                finish(1, m, nc.vector.tensor_copy, nc.sync)
+            else:
+                finish(1, m, nc.scalar.copy, nc.scalar)

from contextlib import ExitStack

import concourse.mybir as mybir

K, T, J, L, N = 512, 1024, 512, 512, 512
FLOPS = 2 * K * N * J + 2 * L * N * J

F32 = mybir.dt.float32
BF16 = mybir.dt.bfloat16
I32 = mybir.dt.int32
U32 = mybir.dt.uint32
U16 = mybir.dt.uint16
U8 = mybir.dt.uint8
FP8X4 = mybir.dt.float8_e4m3fn_x4
FP4X4 = mybir.dt.float4_e2m1fn_x4
SUBTRACT = mybir.AluOpType.subtract

P = 128
PACK = 4
HALF = J // 2
CHUNK = 128
LIST_COLS = HALF // 16


def tile_list_head_changes_in_kernel(
    tc, xf, w_words, w_scales, bx_words, bx_scales, wb_words, wb_scales, offs, offs2, out
):
    nc = tc.nc
    with ExitStack() as ctx:
        sb = ctx.enter_context(tc.tile_pool(name="sb", bufs=1))
        ps = ctx.enter_context(tc.psum_pool(name="ps", bufs=1))

        lists = sb.tile([P, J // 16], U16, name="lists")
        lists2 = sb.tile([P, J // 16], U16, name="lists2")
        x = [sb.tile([P, T], F32, name=f"x{t}") for t in range(PACK)]
        w_codes = sb.tile([P, 2 * N], U8, name="w_codes", align_bytes=64)
        wb_codes = sb.tile([P, 2 * N], U8, name="wb_codes", align_bytes=64)
        w_plane = sb.tile([P, N], U8, name="w_plane", align_bytes=64)
        wb_plane = sb.tile([P, N], U8, name="wb_plane", align_bytes=64)
        bx_plane = sb.tile([P, J], U8, name="bx_plane", align_bytes=64)

        for plane in (wb_plane, bx_plane, w_plane):
            nc.vector.memset(plane[:].bitcast(I32), 0)

        def load_plane(plane, scales):
            for q in range(4):
                nc.sync.dma_start(
                    plane[32 * q : 32 * q + 4, :].bitcast(I32), scales[0, 4 * q : 4 * q + 4, :].bitcast(I32)
                )

        x_rows = xf.rearrange("(p t) c -> p t c", t=PACK)
        nc.sync.dma_start(x[0][:], x_rows[:, 0, :])
        nc.sync.dma_start(lists2[:], offs2)
        nc.sync.dma_start(lists[:], offs)
        nc.sync.dma_start(x[1][:], x_rows[:, 1, :])
        load_plane(wb_plane, wb_scales)
        nc.sync.dma_start(x[2][:], x_rows[:, 2, :])
        load_plane(bx_plane, bx_scales)
        nc.sync.dma_start(x[3][:], x_rows[:, 3, :])
        nc.sync.dma_start(wb_codes[:].bitcast(I32), wb_words[0].bitcast(I32))
        load_plane(w_plane, w_scales)
        nc.sync.dma_start(w_codes[:].bitcast(I32), w_words[0].bitcast(I32))

        def cut(tile, half):
            return tile[:, half * LIST_COLS : (half + 1) * LIST_COLS]

        low0 = sb.tile([P, 2, HALF], F32, name="low0", align_bytes=64)
        shared = sb.tile([P, 3, HALF], F32, name="shared")
        high1 = sb.tile([P, 2, HALF], F32, name="high1")
        pairs = [[low0[:], shared[:, 1:3, :]], [shared[:, 0:2, :], high1[:]]]
        second = [
            [sb.tile([P, HALF], F32, name=f"second0_{t}")[:] for t in range(PACK - 1)] + [high1[:, 0, :]],
            [sb.tile([P, HALF], F32, name=f"second1_{t}")[:] for t in range(PACK - 1)] + [shared[:, 0, :]],
        ]

        def pick_second(half, t):
            nc.vector.tensor_copy(second[half][t], x[t][:].indirect(cut(lists2, half)))

        def change(half, t):
            nc.vector.tensor_tensor(
                pairs[half][t // 2][:, t % 2, :], x[t][:].indirect(cut(lists, half)), second[half][t], SUBTRACT
            )

        woven = [sb.tile([P, HALF, PACK], BF16, name=f"woven{h}", align_bytes=64) for h in range(2)]

        def weave(copy, half, pair, j0, j1):
            src = pairs[half][pair].rearrange("p t j -> p j t")
            copy(woven[half][:, j0:j1, 2 * pair : 2 * pair + 2], src[:, j0:j1, :])

        def quantise(half, j0, j1):
            codes = sb.tile([P, j1 - j0], U32, name=f"d_codes{half}_{j0}", align_bytes=64)
            plane = sb.tile([P, j1 - j0], U8, name=f"d_plane{half}_{j0}", align_bytes=64)
            nc.vector.quantize_mx(
                out=codes[:].bitcast(FP8X4),
                scales=plane[:],
                in_=woven[half][:, j0:j1, :].rearrange("p j t -> p (j t)"),
            )
            return codes, plane

        banks = {(h, m): ps.tile([P, HALF], F32, name=f"bank{h}_{m}") for h in range(2) for m in range(N // P)}

        def product(half, m, c, codes, plane, rhs, rhs_plane, first):
            nc.tensor.matmul_mx(
                out=banks[half, m][:, c * CHUNK : (c + 1) * CHUNK],
                lhsT=codes[:, 2 * P * m : 2 * P * (m + 1)].bitcast(FP4X4),
                lhsT_scale=plane[:, P * m : P * (m + 1)],
                rhs=rhs.bitcast(FP8X4),
                rhs_scale=rhs_plane,
                start=first and c == 0,
                stop=(not first) and c == 1,
            )

        def finish(half, m, copy, queue):
            result = sb.tile([P, HALF], F32, name=f"result{half}_{m}")
            copy(result[:], banks[half, m][:])
            queue.dma_start(out[m * P : (m + 1) * P, half * HALF : (half + 1) * HALF], result[:])

        for t in range(PACK):
            pick_second(0, t)
            pick_second(1, t)
            change(0, t)
            if t % 2 == 1:
                weave(nc.scalar.copy, 0, t // 2, 0, HALF)
        bx_codes = sb.tile([P, J], U32, name="bx_codes", tag="low0", align_bytes=64)
        nc.scalar.dma_start(bx_codes[:].bitcast(I32), bx_words[0].rearrange("p c r -> p (c r)").bitcast(I32))
        for half in range(2):
            for m in range(N // P):
                for c in range(2):
                    cols = slice(half * HALF + c * CHUNK, half * HALF + (c + 1) * CHUNK)
                    product(half, m, c, wb_codes, wb_plane, bx_codes[:, cols], bx_plane[:, cols], True)
        change(1, 3)
        change(1, 2)
        weave(nc.scalar.copy, 1, 1, 0, HALF)
        change(1, 0)
        codes, plane = quantise(0, 0, HALF)
        for m in range(N // P):
            for c in range(2):
                cols = slice(c * CHUNK, (c + 1) * CHUNK)
                product(0, m, c, w_codes, w_plane, codes[:, cols], plane[:, cols], False)
            finish(0, m, nc.scalar.copy, nc.sync)
        change(1, 1)
        for c in range(2):
            weave(nc.vector.tensor_copy, 1, 0, c * CHUNK, (c + 1) * CHUNK)
        last = [quantise(1, c * CHUNK, (c + 1) * CHUNK) for c in range(2)]
        for m in range(N // P):
            for c in range(2):
                product(1, m, c, w_codes, w_plane, last[c][0][:], last[c][1][:], False)
            if m % 2 == 0:
                finish(1, m, nc.vector.tensor_copy, nc.sync)
            else:
                finish(1, m, nc.scalar.copy, nc.scalar)
